import numpy as np
import ml_dtypes


def mxq(x, axis, fmt="e4m3"):
    dtype, down = {"e4m3": (ml_dtypes.float8_e4m3fn, 7), "e5m2": (ml_dtypes.float8_e5m2, 14)}[fmt]
    v = np.moveaxis(np.asarray(x, np.float32).astype(ml_dtypes.bfloat16).astype(np.float64), axis, -1)
    blocks = v.reshape(v.shape[:-1] + (-1, 32))
    amax = np.abs(blocks).max(-1, keepdims=True)
    byte = np.maximum(np.where(amax > 0, np.frexp(amax)[1] - 1 + 127, 0) - down, 1)
    scale = np.exp2(byte - 127.0)
    codes = (blocks / scale).astype(np.float32).astype(dtype).astype(np.float64)
    return np.moveaxis((codes * scale).reshape(v.shape), -1, axis)


WIDE = False


def mx_kscale(k):
    if not WIDE:
        return np.ones(k)
    levels = np.array([10, -10, 5, -5, 0])
    if k % 512:
        return np.exp2(np.random.permutation(np.resize(levels, k // 32))).repeat(32)
    a = np.empty((k // 512, 16))
    for p in range(k // 512):
        a[p, :8] = np.random.permutation(np.resize(levels, 8))
        for g in range(8):
            far = levels[np.abs(levels - a[p, g]) >= 10]
            a[p, g + 8] = far[np.random.randint(len(far))]
    return np.exp2(a.ravel()).repeat(32)


def f64(x):
    return np.asarray(x).astype(np.float64)


def striped(idx):
    return np.tile(idx.reshape(-1, 16).T, (8, 1)).astype(np.uint16)


def unstriped(offs):
    return offs[:16].T.reshape(-1).astype(np.int64)


def pack_weight(w):
    k, n = w.shape
    w = f64(np.asarray(w, np.float32).astype(ml_dtypes.bfloat16)).reshape(k // 32, 32, n)
    amax = np.abs(w).max(1)
    byte = np.clip(np.where(amax > 0, np.frexp(amax)[1] - 1 + 127 - 7, 1), 1, 254)
    scaled = (w * np.exp2(127.0 - byte)[:, None, :]).reshape(k, n).astype(np.float32)
    words = np.ascontiguousarray(scaled.reshape(k // 512, 128, 4, n).transpose(0, 1, 3, 2)).astype(ml_dtypes.float8_e4m3fn).view(np.uint8)
    return words, np.ascontiguousarray(byte.astype(np.uint8).reshape(k // 512, 16, n))


def unpack_weight(words, scales):
    g, p, n, _ = words.shape
    vals = np.ascontiguousarray(words).view(ml_dtypes.float8_e4m3fn).astype(np.float64) * np.repeat(np.exp2(scales.astype(np.float64) - 127.0), 8, axis=1)[..., None]
    return vals.transpose(0, 1, 3, 2).reshape(g * 512, n)


def relu(v):
    return np.maximum(v, 0.0)


def sigmoid(v):
    return 1.0 / (1.0 + np.exp(-np.maximum(v, -700.0)))


K, T, S, N, H = 1024, 1024, 512, 256, 512


def setup_inputs():
    n = np.random.standard_normal
    s = mx_kscale(K)[:, None]
    u = mx_kscale(H)
    packed_xT = pack_weight(n((K, T)) * s)
    return {
        "x_words": packed_xT[0],
        "x_scales": packed_xT[1],
        "w1": (n((K, H)) / np.sqrt(K) / s).astype(np.float32),
        "th1": (-np.random.uniform(0.1, 0.6, (H, 1))).astype(np.float32),
        "unit": (np.random.uniform(0.6, 1.4, (H, 1)) * u[:, None]).astype(np.float32),
        "w2": (n((H, N)) / np.sqrt(H) / u[:, None]).astype(np.float32),
        "offs": striped(np.random.permutation(T)[:S]),
        "par": striped(np.random.permutation(S)),
    }


def reference(x_words, x_scales, w1, th1, unit, w2, offs, par):
    xq = unpack_weight(x_words, x_scales)[:, unstriped(offs)]
    y = mxq(f64(w1), 0, "e4m3").T @ xq
    ft = relu(y + f64(th1))
    fp = ft[:, unstriped(par)]
    child = ft * sigmoid(4.0 * fp - 1.0)
    absb = np.minimum(ft, fp)
    hid = f64(unit) * (child - (0.5 * absb))
    return mxq(f64(w2), 0, "e4m3").T @ mxq(hid, 0, "e4m3")

@@ -1,0 +1,219 @@
+from contextlib import ExitStack
+
+import concourse.mybir as mybir
+
+K, T, S, N, H = 1024, 1024, 512, 256, 512
+FLOPS = 2 * K * H * S + 2 * H * N * S
+
+F32 = mybir.dt.float32
+BF16 = mybir.dt.bfloat16
+I32 = mybir.dt.int32
+U32 = mybir.dt.uint32
+U16 = mybir.dt.uint16
+U8 = mybir.dt.uint8
+FP8X4 = mybir.dt.float8_e4m3fn_x4
+ALU = mybir.AluOpType
+ACT = mybir.ActivationFunctionType
+
+P = 128
+PACK = 4
+K_PASS = P * PACK
+PASSES = K // K_PASS
+HALF = S // 2
+LIST_ROWS = 16
+
+
+def tile_picked_ysaemt_abs_p_kernel(tc, x_words, x_scales, w1, th1, unit, w2, offs, par, out):
+    nc = tc.nc
+    with ExitStack() as ctx:
+        lists = ctx.enter_context(tc.tile_pool(name="lists", bufs=1))
+        sb = ctx.enter_context(tc.tile_pool(name="sb", bufs=1))
+        psum = ctx.enter_context(tc.psum_pool(name="psum", bufs=1))
+
+        offs_sb = lists.tile([P, S // LIST_ROWS], U16, name="offs_sb")
+        par_sb = lists.tile([P, S // LIST_ROWS], U16, name="par_sb")
+
+        scale_table = sb.tile([P, T], U8, name="scale_table", align_bytes=64)
+        nc.gpsimd.memset(scale_table[:].bitcast(I32), 0)
+        minus_one = sb.tile([P, 1], F32, name="minus_one")
+        nc.gpsimd.memset(minus_one[:], -1.0)
+        th_sb = sb.tile([P, PACK], F32, name="th_sb")
+        unit_sb = sb.tile([P, PACK], F32, name="unit_sb")
+        nc.gpsimd.dma_start(out=th_sb[:], in_=th1.rearrange("(p t) o -> p (t o)", t=PACK))
+        nc.gpsimd.dma_start(out=unit_sb[:], in_=unit.rearrange("(p t) o -> p (t o)", t=PACK))
+
+        w1_rows = [w1[o * K_PASS:(o + 1) * K_PASS, :].rearrange("(p j) c -> p j c", j=PACK) for o in range(PASSES)]
+        w1_raw0 = sb.tile([P, PACK, H], F32, name="w1_raw0")
+        word_table = [sb.tile([P, T], U32, name="word_table%d" % o, align_bytes=64) for o in range(PASSES)]
+        w1_raw1 = [sb.tile([P, PACK, H // 2], F32, name="w1_raw1_%d" % h) for h in range(2)]
+
+        def load_words(o):
+            nc.sync.dma_start(out=word_table[o][:].bitcast(I32), in_=x_words[o].rearrange("p n t -> p (n t)").bitcast(I32))
+
+        def load_w1_half(h):
+            nc.sync.dma_start(out=w1_raw1[h][:], in_=w1_rows[1][:, :, h * (H // 2):(h + 1) * (H // 2)])
+
+        nc.sync.dma_start(out=w1_raw0[:], in_=w1_rows[0])
+        nc.sync.dma_start(offs_sb[:], offs)
+        for q in range(4):
+            nc.sync.dma_start(out=scale_table[32 * q:32 * q + 4 * PASSES, :].bitcast(I32), in_=x_scales[:, 4 * q:4 * q + 4, :].bitcast(I32))
+        load_words(0)
+        load_w1_half(0)
+        load_words(1)
+        load_w1_half(1)
+        nc.sync.dma_start(par_sb[:], par)
+        w2_raw = sb.tile([P, PACK, N], F32, name="w2_raw")
+        nc.sync.dma_start(out=w2_raw[:], in_=w2.rearrange("(p j) n -> p j n", j=PACK))
+
+        x_scale = sb.tile([P, S], U8, name="x_scale", align_bytes=64)
+        x_codes = [sb.tile([P, S], U32, name="x_codes0", align_bytes=64)]
+        w1_codes = [sb.tile([P, PACK, P], U32, name="w1_codes%d" % o, align_bytes=64) for o in range(PASSES)]
+        w1_scale = [sb.tile([P, PACK, P], U8, name="w1_scale%d" % o, align_bytes=64) for o in range(PASSES)]
+
+        def deal(copy, raw, t0, t1, name):
+            m = raw.shape[2] // PACK
+            dealt = sb.tile([P, t1 - t0, m, PACK], BF16, name=name, tag=name, align_bytes=64)
+            copy(out=dealt[:].rearrange("p t m j -> p m j t"), in_=raw[:].rearrange("p j (m t) -> p m j t", t=PACK)[:, :, :, t0:t1])
+            return dealt
+
+        dealt0 = deal(nc.scalar.copy, w1_raw0, 0, PACK, "dealt0")
+        nc.vector.tensor_copy(x_scale[:], scale_table[:].indirect(offs_sb[:]))
+        nc.vector.tensor_copy(x_codes[0][:], word_table[0][:].indirect(offs_sb[:]))
+        nc.vector.quantize_mx(out=w1_codes[0][:].rearrange("p t m -> p (t m)").bitcast(FP8X4), scales=w1_scale[0][:].rearrange("p t m -> p (t m)"),
+                              in_=dealt0[:].rearrange("p t m j -> p (t m j)"))
+
+        y = [[psum.tile([P, HALF], F32, name="y%d_%d" % (t, c), tag="bank%d" % (2 * t + c)) for c in range(2)] for t in range(PACK)]
+
+        def product1(o, t, c):
+            cols = slice(c * HALF, (c + 1) * HALF)
+            nc.tensor.matmul_mx(out=y[t][c][:], lhsT=w1_codes[o][:, t, :].bitcast(FP8X4), lhsT_scale=w1_scale[o][:, t, :],
+                                rhs=x_codes[o][:, cols].bitcast(FP8X4), rhs_scale=x_scale[4 * o:P, cols],
+                                start=(o == 0), stop=(o == PASSES - 1))
+
+        for t in range(PACK):
+            for c in range(2):
+                product1(0, t, c)
+
+        def quantize_w1_half(h, t, dealt):
+            ms = slice(h * (P // 2), (h + 1) * (P // 2))
+            nc.vector.quantize_mx(out=w1_codes[1][:, t, ms].bitcast(FP8X4), scales=w1_scale[1][:, t, ms], in_=dealt.rearrange("p m j -> p (m j)"))
+
+        dealt1_0 = deal(nc.scalar.copy, w1_raw1[0], 0, PACK, "dealt1_0")
+        x_codes.append(sb.tile([P, S], U32, name="x_codes1", tag="dealt0", align_bytes=64))
+        nc.vector.tensor_copy(x_codes[1][:], word_table[1][:].indirect(offs_sb[:]))
+        for t in range(PACK):
+            quantize_w1_half(0, t, dealt1_0[:, t, :, :])
+        dealt1_1 = [deal(nc.vector.tensor_copy, w1_raw1[1], 0, 2, "dealt1_1v"), deal(nc.scalar.copy, w1_raw1[1], 2, PACK, "dealt1_1s")]
+        for t in range(PACK):
+            quantize_w1_half(1, t, dealt1_1[t // 2][:, t % 2, :, :])
+        for t in range(PACK):
+            for c in range(2):
+                product1(1, t, c)
+
+        neg_half_unit = sb.tile([P, PACK], F32, name="neg_half_unit")
+        nc.gpsimd.tensor_scalar(neg_half_unit[:], unit_sb[:], -0.5, 0.0, ALU.mult, ALU.add)
+
+        w2_dealt = sb.tile([P, N, PACK], BF16, name="w2_dealt", align_bytes=64)
+        w2_codes = sb.tile([P, N], U32, name="w2_codes", align_bytes=64)
+        w2_scale = sb.tile([P, N], U8, name="w2_scale", align_bytes=64)
+
+        ft = [sb.tile([P, S], F32, name="ft%d" % t, align_bytes=64) for t in range(PACK)]
+
+        def rectify(t, c, on_vector):
+            cols = slice(c * HALF, (c + 1) * HALF)
+            if on_vector:
+                nc.vector.tensor_scalar(ft[t][:, cols], y[t][c][:], th_sb[:, t:t + 1], 0.0, ALU.add, ALU.max)
+            else:
+                nc.scalar.activation(ft[t][:, cols], y[t][c][:], ACT.Relu, bias=th_sb[:, t:t + 1])
+
+        hid = [sb.tile([P, PACK, HALF], BF16, name="hid%d" % c, align_bytes=64) for c in range(2)]
+
+        units = [(t, c) for c in range(2) for t in range(PACK)]
+        fp = [sb.tile([P, HALF], F32, name="fp%d" % u) for u in range(8)]
+        gate = [sb.tile([P, HALF], F32, name="gate%d" % u) for u in range(8)]
+        absb = [sb.tile([P, HALF], F32, name="absb%d" % u) for u in range(8)]
+        child = [sb.tile([P, HALF], F32, name="child%d" % u) for u in range(8)]
+        woven = [sb.tile([P, HALF, PACK], BF16, name="woven%d" % c, align_bytes=64) for c in range(2)]
+
+        def own(u):
+            t, c = units[u]
+            return ft[t][:, c * HALF:(c + 1) * HALF]
+
+        def fetch(u, on_vector):
+            t, c = units[u]
+            parents = ft[t][:].indirect(par_sb[:, c * (HALF // LIST_ROWS):(c + 1) * (HALF // LIST_ROWS)])
+            if on_vector:
+                nc.vector.tensor_copy(fp[u][:], parents)
+            else:
+                nc.scalar.activation(fp[u][:], parents, ACT.Copy)
+
+        def make_gate(u):
+            nc.scalar.activation(gate[u][:], fp[u][:], ACT.Sigmoid, bias=minus_one[:], scale=4.0)
+
+        def make_absb(u):
+            nc.vector.tensor_tensor(absb[u][:], fp[u][:], own(u), ALU.min)
+
+        def make_child(u):
+            t, c = units[u]
+            nc.vector.scalar_tensor_tensor(child[u][:], own(u), unit_sb[:, t:t + 1], gate[u][:], ALU.mult, ALU.mult)
+
+        def make_hid(u):
+            t, c = units[u]
+            nc.vector.scalar_tensor_tensor(hid[c][:, t, :], absb[u][:], neg_half_unit[:, t:t + 1], child[u][:], ALU.mult, ALU.add)
+
+        def weave(copy, c, j0, j1):
+            copy(out=woven[c][:, j0:j1, :].rearrange("p (a i) t -> p a t i", i=2), in_=hid[c][:, :, j0:j1].rearrange("p t (a i) -> p a t i", i=2))
+
+        def product2(c):
+            cols = slice(c * HALF, (c + 1) * HALF)
+            codes = sb.tile([P, HALF], U32, name="hid_codes%d" % c, align_bytes=64)
+            scale = sb.tile([P, HALF], U8, name="hid_scale%d" % c, align_bytes=64)
+            nc.vector.quantize_mx(out=codes[:].bitcast(FP8X4), scales=scale[:], in_=woven[c][:].rearrange("p a t -> p (a t)"))
+            accs = []
+            for b in range(N // P):
+                rows = slice(b * P, (b + 1) * P)
+                acc = psum.tile([P, HALF], F32, name="acc%d_%d" % (c, b), tag="bank%d" % (2 * c + b))
+                nc.tensor.matmul_mx(out=acc[:], lhsT=w2_codes[:, rows].bitcast(FP8X4), lhsT_scale=w2_scale[:, rows],
+                                    rhs=codes[:].bitcast(FP8X4), rhs_scale=scale[:], start=True, stop=True)
+                accs.append(acc)
+            return accs
+
+        def store(copy, c, b, acc):
+            res = sb.tile([P, HALF], F32, name="res%d_%d" % (c, b))
+            copy(res[:], acc[:])
+            nc.sync.dma_start(out=out[b * P:(b + 1) * P, c * HALF:(c + 1) * HALF], in_=res[:])
+
+        nc.gpsimd.tensor_scalar(w2_dealt[:], w2_raw[:].rearrange("p j n -> p n j"), 1.0, 0.0, ALU.mult, ALU.add)
+        rectify(0, 0, False)
+        rectify(0, 1, True)
+        fetch(0, True)
+        rectify(1, 0, False)
+        rectify(1, 1, False)
+        fetch(1, True)
+        make_gate(0)
+        make_absb(0)
+        accs0 = []
+        for u in range(8):
+            if u + 2 < PACK:
+                rectify(u + 2, 0, False)
+                rectify(u + 2, 1, False)
+            make_child(u)
+            if u + 1 < 8:
+                make_gate(u + 1)
+                make_absb(u + 1)
+            if u + 2 < 8:
+                fetch(u + 2, False)
+            make_hid(u)
+            if u == 1:
+                nc.vector.quantize_mx(out=w2_codes[:].bitcast(FP8X4), scales=w2_scale[:], in_=w2_dealt[:].rearrange("p n j -> p (n j)"))
+            if u == 4:
+                weave(nc.vector.tensor_copy, 0, 0, HALF)
+            if u == 5:
+                accs0 = product2(0)
+        for b in range(2):
+            store(nc.scalar.copy, 0, b, accs0[b])
+        weave(nc.vector.tensor_copy, 1, 0, 160)
+        weave(nc.scalar.copy, 1, 160, HALF)
+        accs1 = product2(1)
+        store(nc.scalar.copy, 1, 0, accs1[0])
+        store(nc.vector.tensor_copy, 1, 1, accs1[1])

@@ -21,6 +21,9 @@ K_PASS = P * PACK
 PASSES = K // K_PASS
 HALF = S // 2
 LIST_ROWS = 16
+SPARE = 32
+ALL = slice(0, S)
+HALVES = (slice(0, HALF), slice(HALF, S))
 
 
 def tile_picked_ysaemt_abs_p_kernel(tc, x_words, x_scales, w1, th1, unit, w2, offs, par, out):
@@ -37,142 +40,124 @@ def tile_picked_ysaemt_abs_p_kernel(tc, x_words, x_scales, w1, th1, unit, w2, of
         nc.gpsimd.memset(scale_table[:].bitcast(I32), 0)
         minus_one = sb.tile([P, 1], F32, name="minus_one")
         nc.gpsimd.memset(minus_one[:], -1.0)
+        warm = sb.tile([P, 1], F32, name="warm")
+        nc.scalar.activation(warm[:], minus_one[:], ACT.Sigmoid, bias=minus_one[:], scale=4.0)
+        ft = [sb.tile([P, S + SPARE], F32, name="ft%d" % t, align_bytes=64) for t in range(PACK)]
+        for t in range(PACK):
+            nc.gpsimd.memset(ft[t][:, S:], 0.0)
         th_sb = sb.tile([P, PACK], F32, name="th_sb")
         unit_sb = sb.tile([P, PACK], F32, name="unit_sb")
         nc.gpsimd.dma_start(out=th_sb[:], in_=th1.rearrange("(p t) o -> p (t o)", t=PACK))
         nc.gpsimd.dma_start(out=unit_sb[:], in_=unit.rearrange("(p t) o -> p (t o)", t=PACK))
+        neg_half_unit = sb.tile([P, PACK], F32, name="neg_half_unit")
+        nc.gpsimd.tensor_scalar(neg_half_unit[:], unit_sb[:], -0.5, 0.0, ALU.mult, ALU.add)
 
         w1_rows = [w1[o * K_PASS:(o + 1) * K_PASS, :].rearrange("(p j) c -> p j c", j=PACK) for o in range(PASSES)]
         w1_raw0 = sb.tile([P, PACK, H], F32, name="w1_raw0")
         word_table = [sb.tile([P, T], U32, name="word_table%d" % o, align_bytes=64) for o in range(PASSES)]
         w1_raw1 = [sb.tile([P, PACK, H // 2], F32, name="w1_raw1_%d" % h) for h in range(2)]
+        w2_raw = sb.tile([P, PACK, N], F32, name="w2_raw")
 
         def load_words(o):
             nc.sync.dma_start(out=word_table[o][:].bitcast(I32), in_=x_words[o].rearrange("p n t -> p (n t)").bitcast(I32))
 
-        def load_w1_half(h):
-            nc.sync.dma_start(out=w1_raw1[h][:], in_=w1_rows[1][:, :, h * (H // 2):(h + 1) * (H // 2)])
-
-        nc.sync.dma_start(out=w1_raw0[:], in_=w1_rows[0])
+        load_words(0)
         nc.sync.dma_start(offs_sb[:], offs)
         for q in range(4):
             nc.sync.dma_start(out=scale_table[32 * q:32 * q + 4 * PASSES, :].bitcast(I32), in_=x_scales[:, 4 * q:4 * q + 4, :].bitcast(I32))
-        load_words(0)
-        load_w1_half(0)
+        nc.sync.dma_start(out=w1_raw0[:], in_=w1_rows[0])
         load_words(1)
-        load_w1_half(1)
+        for h in range(2):
+            nc.sync.dma_start(out=w1_raw1[h][:], in_=w1_rows[1][:, :, h * (H // 2):(h + 1) * (H // 2)])
         nc.sync.dma_start(par_sb[:], par)
-        w2_raw = sb.tile([P, PACK, N], F32, name="w2_raw")
         nc.sync.dma_start(out=w2_raw[:], in_=w2.rearrange("(p j) n -> p j n", j=PACK))
 
         x_scale = sb.tile([P, S], U8, name="x_scale", align_bytes=64)
-        x_codes = [sb.tile([P, S], U32, name="x_codes0", align_bytes=64)]
+        x_codes = [sb.tile([P, S], U32, name="x_codes%d" % o, align_bytes=64) for o in range(PASSES)]
         w1_codes = [sb.tile([P, PACK, P], U32, name="w1_codes%d" % o, align_bytes=64) for o in range(PASSES)]
         w1_scale = [sb.tile([P, PACK, P], U8, name="w1_scale%d" % o, align_bytes=64) for o in range(PASSES)]
 
-        def deal(copy, raw, t0, t1, name):
+        def deal(raw, name):
             m = raw.shape[2] // PACK
-            dealt = sb.tile([P, t1 - t0, m, PACK], BF16, name=name, tag=name, align_bytes=64)
-            copy(out=dealt[:].rearrange("p t m j -> p m j t"), in_=raw[:].rearrange("p j (m t) -> p m j t", t=PACK)[:, :, :, t0:t1])
+            source = raw[:].rearrange("p j (m t) -> p m j t", t=PACK)
+            dealt = []
+            for pair, copy in enumerate((nc.vector.tensor_copy, nc.scalar.copy)):
+                half = sb.tile([P, 2, m, PACK], BF16, name="%s_%d" % (name, pair), align_bytes=64)
+                copy(out=half[:].rearrange("p t m j -> p m j t"), in_=source[:, :, :, 2 * pair:2 * pair + 2])
+                dealt.append(half)
             return dealt
 
-        dealt0 = deal(nc.scalar.copy, w1_raw0, 0, PACK, "dealt0")
-        nc.vector.tensor_copy(x_scale[:], scale_table[:].indirect(offs_sb[:]))
         nc.vector.tensor_copy(x_codes[0][:], word_table[0][:].indirect(offs_sb[:]))
-        nc.vector.quantize_mx(out=w1_codes[0][:].rearrange("p t m -> p (t m)").bitcast(FP8X4), scales=w1_scale[0][:].rearrange("p t m -> p (t m)"),
-                              in_=dealt0[:].rearrange("p t m j -> p (t m j)"))
-
-        y = [[psum.tile([P, HALF], F32, name="y%d_%d" % (t, c), tag="bank%d" % (2 * t + c)) for c in range(2)] for t in range(PACK)]
-
-        def product1(o, t, c):
-            cols = slice(c * HALF, (c + 1) * HALF)
-            nc.tensor.matmul_mx(out=y[t][c][:], lhsT=w1_codes[o][:, t, :].bitcast(FP8X4), lhsT_scale=w1_scale[o][:, t, :],
-                                rhs=x_codes[o][:, cols].bitcast(FP8X4), rhs_scale=x_scale[4 * o:P, cols],
-                                start=(o == 0), stop=(o == PASSES - 1))
-
-        for t in range(PACK):
-            for c in range(2):
-                product1(0, t, c)
-
-        def quantize_w1_half(h, t, dealt):
-            ms = slice(h * (P // 2), (h + 1) * (P // 2))
-            nc.vector.quantize_mx(out=w1_codes[1][:, t, ms].bitcast(FP8X4), scales=w1_scale[1][:, t, ms], in_=dealt.rearrange("p m j -> p (m j)"))
-
-        dealt1_0 = deal(nc.scalar.copy, w1_raw1[0], 0, PACK, "dealt1_0")
-        x_codes.append(sb.tile([P, S], U32, name="x_codes1", tag="dealt0", align_bytes=64))
+        nc.vector.tensor_copy(x_scale[:], scale_table[:].indirect(offs_sb[:]))
+        dealt0 = deal(w1_raw0, "dealt0")
+        for pair in range(2):
+            ts = slice(2 * pair, 2 * pair + 2)
+            nc.vector.quantize_mx(out=w1_codes[0][:, ts, :].rearrange("p t m -> p (t m)").bitcast(FP8X4),
+                                  scales=w1_scale[0][:, ts, :].rearrange("p t m -> p (t m)"),
+                                  in_=dealt0[pair][:].rearrange("p t m j -> p (t m j)"))
         nc.vector.tensor_copy(x_codes[1][:], word_table[1][:].indirect(offs_sb[:]))
-        for t in range(PACK):
-            quantize_w1_half(0, t, dealt1_0[:, t, :, :])
-        dealt1_1 = [deal(nc.vector.tensor_copy, w1_raw1[1], 0, 2, "dealt1_1v"), deal(nc.scalar.copy, w1_raw1[1], 2, PACK, "dealt1_1s")]
-        for t in range(PACK):
-            quantize_w1_half(1, t, dealt1_1[t // 2][:, t % 2, :, :])
-        for t in range(PACK):
-            for c in range(2):
-                product1(1, t, c)
 
-        neg_half_unit = sb.tile([P, PACK], F32, name="neg_half_unit")
-        nc.gpsimd.tensor_scalar(neg_half_unit[:], unit_sb[:], -0.5, 0.0, ALU.mult, ALU.add)
+        pieces = [(0, HALVES[0]), (0, HALVES[1])] + [(t, ALL) for t in range(1, PACK)]
+        y = [psum.tile([P, cols.stop - cols.start], F32, name="y%d" % i, tag="y%d" % i) for i, (t, cols) in enumerate(pieces)]
+
+        def product1(o):
+            for i, (t, cols) in enumerate(pieces):
+                nc.tensor.matmul_mx(out=y[i][:], lhsT=w1_codes[o][:, t, :].bitcast(FP8X4), lhsT_scale=w1_scale[o][:, t, :],
+                                    rhs=x_codes[o][:, cols].bitcast(FP8X4), rhs_scale=x_scale[4 * o:P, cols],
+                                    start=(o == 0), stop=(o == PASSES - 1))
+
+        product1(0)
+        for h in range(2):
+            dealt1 = deal(w1_raw1[h], "dealt1_%d" % h)
+            ms = slice(h * (P // 2), (h + 1) * (P // 2))
+            for t in range(PACK):
+                nc.vector.quantize_mx(out=w1_codes[1][:, t, ms].bitcast(FP8X4), scales=w1_scale[1][:, t, ms],
+                                      in_=dealt1[t // 2][:, t % 2, :, :].rearrange("p m j -> p (m j)"))
+        product1(1)
 
         w2_dealt = sb.tile([P, N, PACK], BF16, name="w2_dealt", align_bytes=64)
         w2_codes = sb.tile([P, N], U32, name="w2_codes", align_bytes=64)
         w2_scale = sb.tile([P, N], U8, name="w2_scale", align_bytes=64)
 
-        ft = [sb.tile([P, S], F32, name="ft%d" % t, align_bytes=64) for t in range(PACK)]
+        fp = [sb.tile([P, S], F32, name="fp%d" % t) for t in range(PACK)]
+        gate = [sb.tile([P, S], F32, name="gate%d" % t) for t in range(PACK)]
+        absb = [sb.tile([P, S], F32, name="absb%d" % t) for t in range(PACK)]
+        child = [sb.tile([P, S], F32, name="child%d" % t) for t in range(PACK)]
+        hid = sb.tile([P, PACK, S], BF16, name="hid", align_bytes=64)
 
-        def rectify(t, c, on_vector):
-            cols = slice(c * HALF, (c + 1) * HALF)
+        def rectify(i, on_vector):
+            t, cols = pieces[i]
             if on_vector:
-                nc.vector.tensor_scalar(ft[t][:, cols], y[t][c][:], th_sb[:, t:t + 1], 0.0, ALU.add, ALU.max)
+                nc.vector.tensor_scalar(ft[t][:, cols], y[i][:], th_sb[:, t:t + 1], 0.0, ALU.add, ALU.max)
             else:
-                nc.scalar.activation(ft[t][:, cols], y[t][c][:], ACT.Relu, bias=th_sb[:, t:t + 1])
+                nc.scalar.activation(ft[t][:, cols], y[i][:], ACT.Relu, bias=th_sb[:, t:t + 1])
 
-        hid = [sb.tile([P, PACK, HALF], BF16, name="hid%d" % c, align_bytes=64) for c in range(2)]
+        def fetch_and_gate(t):
+            nc.scalar.activation(fp[t][:], ft[t][:].indirect(par_sb[:]), ACT.Copy)
+            nc.scalar.activation(gate[t][:], fp[t][:], ACT.Sigmoid, bias=minus_one[:], scale=4.0)
 
-        units = [(t, c) for c in range(2) for t in range(PACK)]
-        fp = [sb.tile([P, HALF], F32, name="fp%d" % u) for u in range(8)]
-        gate = [sb.tile([P, HALF], F32, name="gate%d" % u) for u in range(8)]
-        absb = [sb.tile([P, HALF], F32, name="absb%d" % u) for u in range(8)]
-        child = [sb.tile([P, HALF], F32, name="child%d" % u) for u in range(8)]
-        woven = [sb.tile([P, HALF, PACK], BF16, name="woven%d" % c, align_bytes=64) for c in range(2)]
+        def make_absb(t, cols):
+            nc.vector.tensor_tensor(absb[t][:, cols], fp[t][:, cols], ft[t][:, cols], ALU.min)
 
-        def own(u):
-            t, c = units[u]
-            return ft[t][:, c * HALF:(c + 1) * HALF]
+        def make_child(t, cols):
+            nc.vector.scalar_tensor_tensor(child[t][:, cols], ft[t][:, cols], unit_sb[:, t:t + 1], gate[t][:, cols], ALU.mult, ALU.mult)
 
-        def fetch(u, on_vector):
-            t, c = units[u]
-            parents = ft[t][:].indirect(par_sb[:, c * (HALF // LIST_ROWS):(c + 1) * (HALF // LIST_ROWS)])
-            if on_vector:
-                nc.vector.tensor_copy(fp[u][:], parents)
-            else:
-                nc.scalar.activation(fp[u][:], parents, ACT.Copy)
+        def make_hid(t, cols):
+            nc.vector.scalar_tensor_tensor(hid[:, t, cols], absb[t][:, cols], neg_half_unit[:, t:t + 1], child[t][:, cols], ALU.mult, ALU.add)
 
-        def make_gate(u):
-            nc.scalar.activation(gate[u][:], fp[u][:], ACT.Sigmoid, bias=minus_one[:], scale=4.0)
+        def weave(copy, c):
+            woven = sb.tile([P, HALF, PACK], BF16, name="woven%d" % c, align_bytes=64)
+            copy(out=woven[:].rearrange("p (a i) t -> p a t i", i=2), in_=hid[:, :, HALVES[c]].rearrange("p t (a i) -> p a t i", i=2))
+            return woven
 
-        def make_absb(u):
-            nc.vector.tensor_tensor(absb[u][:], fp[u][:], own(u), ALU.min)
-
-        def make_child(u):
-            t, c = units[u]
-            nc.vector.scalar_tensor_tensor(child[u][:], own(u), unit_sb[:, t:t + 1], gate[u][:], ALU.mult, ALU.mult)
-
-        def make_hid(u):
-            t, c = units[u]
-            nc.vector.scalar_tensor_tensor(hid[c][:, t, :], absb[u][:], neg_half_unit[:, t:t + 1], child[u][:], ALU.mult, ALU.add)
-
-        def weave(copy, c, j0, j1):
-            copy(out=woven[c][:, j0:j1, :].rearrange("p (a i) t -> p a t i", i=2), in_=hid[c][:, :, j0:j1].rearrange("p t (a i) -> p a t i", i=2))
-
-        def product2(c):
-            cols = slice(c * HALF, (c + 1) * HALF)
+        def product2(c, woven):
             codes = sb.tile([P, HALF], U32, name="hid_codes%d" % c, align_bytes=64)
             scale = sb.tile([P, HALF], U8, name="hid_scale%d" % c, align_bytes=64)
-            nc.vector.quantize_mx(out=codes[:].bitcast(FP8X4), scales=scale[:], in_=woven[c][:].rearrange("p a t -> p (a t)"))
+            nc.vector.quantize_mx(out=codes[:].bitcast(FP8X4), scales=scale[:], in_=woven[:].rearrange("p a t -> p (a t)"))
             accs = []
             for b in range(N // P):
                 rows = slice(b * P, (b + 1) * P)
-                acc = psum.tile([P, HALF], F32, name="acc%d_%d" % (c, b), tag="bank%d" % (2 * c + b))
+                acc = psum.tile([P, HALF], F32, name="acc%d_%d" % (c, b), tag="y%d" % (2 * c + b))
                 nc.tensor.matmul_mx(out=acc[:], lhsT=w2_codes[:, rows].bitcast(FP8X4), lhsT_scale=w2_scale[:, rows],
                                     rhs=codes[:].bitcast(FP8X4), rhs_scale=scale[:], start=True, stop=True)
                 accs.append(acc)
@@ -181,39 +166,37 @@ def tile_picked_ysaemt_abs_p_kernel(tc, x_words, x_scales, w1, th1, unit, w2, of
         def store(copy, c, b, acc):
             res = sb.tile([P, HALF], F32, name="res%d_%d" % (c, b))
             copy(res[:], acc[:])
-            nc.sync.dma_start(out=out[b * P:(b + 1) * P, c * HALF:(c + 1) * HALF], in_=res[:])
+            nc.sync.dma_start(out=out[b * P:(b + 1) * P, HALVES[c]], in_=res[:])
 
         nc.gpsimd.tensor_scalar(w2_dealt[:], w2_raw[:].rearrange("p j n -> p n j"), 1.0, 0.0, ALU.mult, ALU.add)
-        rectify(0, 0, False)
-        rectify(0, 1, True)
-        fetch(0, True)
-        rectify(1, 0, False)
-        rectify(1, 1, False)
-        fetch(1, True)
-        make_gate(0)
-        make_absb(0)
-        accs0 = []
-        for u in range(8):
-            if u + 2 < PACK:
-                rectify(u + 2, 0, False)
-                rectify(u + 2, 1, False)
-            make_child(u)
-            if u + 1 < 8:
-                make_gate(u + 1)
-                make_absb(u + 1)
-            if u + 2 < 8:
-                fetch(u + 2, False)
-            make_hid(u)
-            if u == 1:
-                nc.vector.quantize_mx(out=w2_codes[:].bitcast(FP8X4), scales=w2_scale[:], in_=w2_dealt[:].rearrange("p n j -> p (n j)"))
-            if u == 4:
-                weave(nc.vector.tensor_copy, 0, 0, HALF)
-            if u == 5:
-                accs0 = product2(0)
-        for b in range(2):
-            store(nc.scalar.copy, 0, b, accs0[b])
-        weave(nc.vector.tensor_copy, 1, 0, 160)
-        weave(nc.scalar.copy, 1, 160, HALF)
-        accs1 = product2(1)
-        store(nc.scalar.copy, 1, 0, accs1[0])
-        store(nc.vector.tensor_copy, 1, 1, accs1[1])
+        rectify(0, False)
+        rectify(1, True)
+        fetch_and_gate(0)
+        rectify(2, True)
+        rectify(3, True)
+        fetch_and_gate(1)
+        fetch_and_gate(2)
+        make_absb(0, ALL)
+        make_child(0, ALL)
+        rectify(4, True)
+        fetch_and_gate(3)
+        make_hid(0, ALL)
+        make_absb(1, ALL)
+        make_child(1, ALL)
+        nc.vector.quantize_mx(out=w2_codes[:].bitcast(FP8X4), scales=w2_scale[:], in_=w2_dealt[:].rearrange("p n j -> p (n j)"))
+        make_hid(1, ALL)
+        make_absb(2, ALL)
+        make_child(2, ALL)
+        make_absb(3, HALVES[0])
+        make_hid(2, ALL)
+        make_child(3, HALVES[0])
+        make_absb(3, HALVES[1])
+        make_hid(3, HALVES[0])
+        woven0 = weave(nc.scalar.copy, 0)
+        make_child(3, HALVES[1])
+        make_hid(3, HALVES[1])
+        woven1 = weave(nc.vector.tensor_copy, 1)
+        accs = [product2(0, woven0), product2(1, woven1)]
+        for c in range(2):
+            store(nc.scalar.copy, c, 0, accs[c][0])
+            store(nc.vector.tensor_copy, c, 1, accs[c][1])

@@ -21,7 +21,6 @@ K_PASS = P * PACK
 PASSES = K // K_PASS
 HALF = S // 2
 LIST_ROWS = 16
-SPARE = 32
 ALL = slice(0, S)
 HALVES = (slice(0, HALF), slice(HALF, S))
 
@@ -42,9 +41,7 @@ def tile_picked_ysaemt_abs_p_kernel(tc, x_words, x_scales, w1, th1, unit, w2, of
         nc.gpsimd.memset(minus_one[:], -1.0)
         warm = sb.tile([P, 1], F32, name="warm")
         nc.scalar.activation(warm[:], minus_one[:], ACT.Sigmoid, bias=minus_one[:], scale=4.0)
-        ft = [sb.tile([P, S + SPARE], F32, name="ft%d" % t, align_bytes=64) for t in range(PACK)]
-        for t in range(PACK):
-            nc.gpsimd.memset(ft[t][:, S:], 0.0)
+        ft = [sb.tile([P, S], F32, name="ft%d" % t, align_bytes=64) for t in range(PACK)]
         th_sb = sb.tile([P, PACK], F32, name="th_sb")
         unit_sb = sb.tile([P, PACK], F32, name="unit_sb")
         nc.gpsimd.dma_start(out=th_sb[:], in_=th1.rearrange("(p t) o -> p (t o)", t=PACK))
@@ -115,12 +112,11 @@ def tile_picked_ysaemt_abs_p_kernel(tc, x_words, x_scales, w1, th1, unit, w2, of
                                       in_=dealt1[t // 2][:, t % 2, :, :].rearrange("p m j -> p (m j)"))
         product1(1)
 
-        w2_dealt = sb.tile([P, N, PACK], BF16, name="w2_dealt", align_bytes=64)
         w2_codes = sb.tile([P, N], U32, name="w2_codes", align_bytes=64)
         w2_scale = sb.tile([P, N], U8, name="w2_scale", align_bytes=64)
 
         fp = [sb.tile([P, S], F32, name="fp%d" % t) for t in range(PACK)]
-        gate = [sb.tile([P, S], F32, name="gate%d" % t) for t in range(PACK)]
+        gate = [sb.tile([P, S], F32, name="gate%d" % t, tag="gate%d" % t, align_bytes=64) for t in range(PACK)]
         absb = [sb.tile([P, S], F32, name="absb%d" % t) for t in range(PACK)]
         child = [sb.tile([P, S], F32, name="child%d" % t) for t in range(PACK)]
         hid = sb.tile([P, PACK, S], BF16, name="hid", align_bytes=64)
@@ -133,8 +129,14 @@ def tile_picked_ysaemt_abs_p_kernel(tc, x_words, x_scales, w1, th1, unit, w2, of
                 nc.scalar.activation(ft[t][:, cols], y[i][:], ACT.Relu, bias=th_sb[:, t:t + 1])
 
         def fetch_and_gate(t):
-            nc.scalar.activation(fp[t][:], ft[t][:].indirect(par_sb[:]), ACT.Copy)
-            nc.scalar.activation(gate[t][:], fp[t][:], ACT.Sigmoid, bias=minus_one[:], scale=4.0)
+            for cols in HALVES:
+                parents = ft[t][:].indirect(par_sb[:, cols.start // LIST_ROWS:cols.stop // LIST_ROWS])
+                if t == 0 and cols == HALVES[1]:
+                    nc.vector.tensor_copy(fp[t][:, cols], parents)
+                else:
+                    nc.scalar.activation(fp[t][:, cols], parents, ACT.Copy)
+            for cols in HALVES:
+                nc.scalar.activation(gate[t][:, cols], fp[t][:, cols], ACT.Sigmoid, bias=minus_one[:], scale=4.0)
 
         def make_absb(t, cols):
             nc.vector.tensor_tensor(absb[t][:, cols], fp[t][:, cols], ft[t][:, cols], ALU.min)
@@ -168,35 +170,36 @@ def tile_picked_ysaemt_abs_p_kernel(tc, x_words, x_scales, w1, th1, unit, w2, of
             copy(res[:], acc[:])
             nc.sync.dma_start(out=out[b * P:(b + 1) * P, HALVES[c]], in_=res[:])
 
-        nc.gpsimd.tensor_scalar(w2_dealt[:], w2_raw[:].rearrange("p j n -> p n j"), 1.0, 0.0, ALU.mult, ALU.add)
         rectify(0, False)
         rectify(1, True)
         fetch_and_gate(0)
         rectify(2, True)
-        rectify(3, True)
         fetch_and_gate(1)
-        fetch_and_gate(2)
         make_absb(0, ALL)
         make_child(0, ALL)
-        rectify(4, True)
+        rectify(3, True)
+        rectify(4, False)
+        fetch_and_gate(2)
         fetch_and_gate(3)
         make_hid(0, ALL)
         make_absb(1, ALL)
         make_child(1, ALL)
-        nc.vector.quantize_mx(out=w2_codes[:].bitcast(FP8X4), scales=w2_scale[:], in_=w2_dealt[:].rearrange("p n j -> p (n j)"))
-        make_hid(1, ALL)
         make_absb(2, ALL)
+        make_hid(1, ALL)
         make_child(2, ALL)
-        make_absb(3, HALVES[0])
-        make_hid(2, ALL)
-        make_child(3, HALVES[0])
-        make_absb(3, HALVES[1])
-        make_hid(3, HALVES[0])
-        woven0 = weave(nc.scalar.copy, 0)
-        make_child(3, HALVES[1])
-        make_hid(3, HALVES[1])
-        woven1 = weave(nc.vector.tensor_copy, 1)
-        accs = [product2(0, woven0), product2(1, woven1)]
+        w2_dealt = sb.tile([P, N, PACK], BF16, name="w2_dealt", tag="gate2", align_bytes=64)
+        nc.scalar.copy(out=w2_dealt[:].rearrange("p (a i) j -> p a j i", i=2), in_=w2_raw[:].rearrange("p j (a i) -> p a j i", i=2))
+        make_absb(3, ALL)
+        woven = []
+        for c in range(2):
+            make_child(3, HALVES[c])
+            make_hid(2, HALVES[c])
+            make_hid(3, HALVES[c])
+            if c == 0:
+                woven.append(weave(nc.scalar.copy, 0))
+        nc.vector.quantize_mx(out=w2_codes[:].bitcast(FP8X4), scales=w2_scale[:], in_=w2_dealt[:].rearrange("p n j -> p (n j)"))
+        woven.append(weave(nc.vector.tensor_copy, 1))
+        accs = [product2(c, woven[c]) for c in range(2)]
         for c in range(2):
             store(nc.scalar.copy, c, 0, accs[c][0])
             store(nc.vector.tensor_copy, c, 1, accs[c][1])

@@ -19,8 +19,12 @@ P = 128
 PACK = 4
 K_PASS = P * PACK
 PASSES = K // K_PASS
-HALF = S // 2
+QUADRANT = 32
+SCALE_ROWS = 4
 LIST_ROWS = 16
+SPARE = 32
+RUN = 4
+HALF = S // 2
 ALL = slice(0, S)
 HALVES = (slice(0, HALF), slice(HALF, S))
 
@@ -41,7 +45,9 @@ def tile_picked_ysaemt_abs_p_kernel(tc, x_words, x_scales, w1, th1, unit, w2, of
         nc.gpsimd.memset(minus_one[:], -1.0)
         warm = sb.tile([P, 1], F32, name="warm")
         nc.scalar.activation(warm[:], minus_one[:], ACT.Sigmoid, bias=minus_one[:], scale=4.0)
-        ft = [sb.tile([P, S], F32, name="ft%d" % t, align_bytes=64) for t in range(PACK)]
+        ft = [sb.tile([P, S + (SPARE if t else 0)], F32, name="ft%d" % t, align_bytes=64) for t in range(PACK)]
+        for t in range(1, PACK):
+            nc.gpsimd.memset(ft[t][:, S:], 0.0)
         th_sb = sb.tile([P, PACK], F32, name="th_sb")
         unit_sb = sb.tile([P, PACK], F32, name="unit_sb")
         nc.gpsimd.dma_start(out=th_sb[:], in_=th1.rearrange("(p t) o -> p (t o)", t=PACK))
@@ -60,8 +66,9 @@ def tile_picked_ysaemt_abs_p_kernel(tc, x_words, x_scales, w1, th1, unit, w2, of
 
         load_words(0)
         nc.sync.dma_start(offs_sb[:], offs)
-        for q in range(4):
-            nc.sync.dma_start(out=scale_table[32 * q:32 * q + 4 * PASSES, :].bitcast(I32), in_=x_scales[:, 4 * q:4 * q + 4, :].bitcast(I32))
+        for q in range(P // QUADRANT):
+            nc.sync.dma_start(out=scale_table[QUADRANT * q:QUADRANT * q + SCALE_ROWS * PASSES, :].bitcast(I32),
+                              in_=x_scales[:, SCALE_ROWS * q:SCALE_ROWS * (q + 1), :].bitcast(I32))
         nc.sync.dma_start(out=w1_raw0[:], in_=w1_rows[0])
         load_words(1)
         for h in range(2):
@@ -79,18 +86,18 @@ def tile_picked_ysaemt_abs_p_kernel(tc, x_words, x_scales, w1, th1, unit, w2, of
             source = raw[:].rearrange("p j (m t) -> p m j t", t=PACK)
             dealt = []
             for pair, copy in enumerate((nc.vector.tensor_copy, nc.scalar.copy)):
-                half = sb.tile([P, 2, m, PACK], BF16, name="%s_%d" % (name, pair), align_bytes=64)
-                copy(out=half[:].rearrange("p t m j -> p m j t"), in_=source[:, :, :, 2 * pair:2 * pair + 2])
-                dealt.append(half)
+                two_slots = sb.tile([P, 2, m, PACK], BF16, name="%s_%d" % (name, pair), align_bytes=64)
+                copy(out=two_slots[:].rearrange("p t m j -> p m j t"), in_=source[:, :, :, 2 * pair:2 * pair + 2])
+                dealt.append(two_slots)
             return dealt
 
         nc.vector.tensor_copy(x_codes[0][:], word_table[0][:].indirect(offs_sb[:]))
         nc.vector.tensor_copy(x_scale[:], scale_table[:].indirect(offs_sb[:]))
         dealt0 = deal(w1_raw0, "dealt0")
         for pair in range(2):
-            ts = slice(2 * pair, 2 * pair + 2)
-            nc.vector.quantize_mx(out=w1_codes[0][:, ts, :].rearrange("p t m -> p (t m)").bitcast(FP8X4),
-                                  scales=w1_scale[0][:, ts, :].rearrange("p t m -> p (t m)"),
+            slots = slice(2 * pair, 2 * pair + 2)
+            nc.vector.quantize_mx(out=w1_codes[0][:, slots, :].rearrange("p t m -> p (t m)").bitcast(FP8X4),
+                                  scales=w1_scale[0][:, slots, :].rearrange("p t m -> p (t m)"),
                                   in_=dealt0[pair][:].rearrange("p t m j -> p (t m j)"))
         nc.vector.tensor_copy(x_codes[1][:], word_table[1][:].indirect(offs_sb[:]))
 
@@ -100,7 +107,7 @@ def tile_picked_ysaemt_abs_p_kernel(tc, x_words, x_scales, w1, th1, unit, w2, of
         def product1(o):
             for i, (t, cols) in enumerate(pieces):
                 nc.tensor.matmul_mx(out=y[i][:], lhsT=w1_codes[o][:, t, :].bitcast(FP8X4), lhsT_scale=w1_scale[o][:, t, :],
-                                    rhs=x_codes[o][:, cols].bitcast(FP8X4), rhs_scale=x_scale[4 * o:P, cols],
+                                    rhs=x_codes[o][:, cols].bitcast(FP8X4), rhs_scale=x_scale[SCALE_ROWS * o:P, cols],
                                     start=(o == 0), stop=(o == PASSES - 1))
 
         product1(0)
@@ -116,10 +123,11 @@ def tile_picked_ysaemt_abs_p_kernel(tc, x_words, x_scales, w1, th1, unit, w2, of
         w2_scale = sb.tile([P, N], U8, name="w2_scale", align_bytes=64)
 
         fp = [sb.tile([P, S], F32, name="fp%d" % t) for t in range(PACK)]
-        gate = [sb.tile([P, S], F32, name="gate%d" % t, tag="gate%d" % t, align_bytes=64) for t in range(PACK)]
+        gate = [sb.tile([P, S], F32, name="gate%d" % t) for t in range(PACK)]
         absb = [sb.tile([P, S], F32, name="absb%d" % t) for t in range(PACK)]
         child = [sb.tile([P, S], F32, name="child%d" % t) for t in range(PACK)]
-        hid = sb.tile([P, PACK, S], BF16, name="hid", align_bytes=64)
+        hid = sb.tile([P, 2, PACK, HALF], BF16, name="hid", align_bytes=64)
+        w2_dealt = sb.tile([P, N, PACK], BF16, name="w2_dealt", align_bytes=64)
 
         def rectify(i, on_vector):
             t, cols = pieces[i]
@@ -129,14 +137,13 @@ def tile_picked_ysaemt_abs_p_kernel(tc, x_words, x_scales, w1, th1, unit, w2, of
                 nc.scalar.activation(ft[t][:, cols], y[i][:], ACT.Relu, bias=th_sb[:, t:t + 1])
 
         def fetch_and_gate(t):
-            for cols in HALVES:
-                parents = ft[t][:].indirect(par_sb[:, cols.start // LIST_ROWS:cols.stop // LIST_ROWS])
-                if t == 0 and cols == HALVES[1]:
-                    nc.vector.tensor_copy(fp[t][:, cols], parents)
-                else:
-                    nc.scalar.activation(fp[t][:, cols], parents, ACT.Copy)
-            for cols in HALVES:
-                nc.scalar.activation(gate[t][:, cols], fp[t][:, cols], ACT.Sigmoid, bias=minus_one[:], scale=4.0)
+            if t == 0:
+                list_cols = HALF // LIST_ROWS
+                nc.scalar.activation(fp[t][:, HALVES[0]], ft[t][:].indirect(par_sb[:, :list_cols]), ACT.Copy)
+                nc.vector.tensor_copy(fp[t][:, HALVES[1]], ft[t][:].indirect(par_sb[:, list_cols:]))
+            else:
+                nc.scalar.activation(fp[t][:], ft[t][:].indirect(par_sb[:]), ACT.Copy)
+            nc.scalar.activation(gate[t][:], fp[t][:], ACT.Sigmoid, bias=minus_one[:], scale=4.0)
 
         def make_absb(t, cols):
             nc.vector.tensor_tensor(absb[t][:, cols], fp[t][:, cols], ft[t][:, cols], ALU.min)
@@ -145,61 +152,61 @@ def tile_picked_ysaemt_abs_p_kernel(tc, x_words, x_scales, w1, th1, unit, w2, of
             nc.vector.scalar_tensor_tensor(child[t][:, cols], ft[t][:, cols], unit_sb[:, t:t + 1], gate[t][:, cols], ALU.mult, ALU.mult)
 
         def make_hid(t, cols):
-            nc.vector.scalar_tensor_tensor(hid[:, t, cols], absb[t][:, cols], neg_half_unit[:, t:t + 1], child[t][:, cols], ALU.mult, ALU.add)
+            halves = slice(cols.start // HALF, cols.stop // HALF)
+            nc.vector.scalar_tensor_tensor(hid[:, halves, t, :], absb[t][:, cols].rearrange("p (c j) -> p c j", j=HALF), neg_half_unit[:, t:t + 1],
+                                           child[t][:, cols].rearrange("p (c j) -> p c j", j=HALF), ALU.mult, ALU.add)
 
         def weave(copy, c):
-            woven = sb.tile([P, HALF, PACK], BF16, name="woven%d" % c, align_bytes=64)
-            copy(out=woven[:].rearrange("p (a i) t -> p a t i", i=2), in_=hid[:, :, HALVES[c]].rearrange("p t (a i) -> p a t i", i=2))
-            return woven
+            woven_half = sb.tile([P, HALF, PACK], BF16, name="woven%d" % c, align_bytes=64)
+            copy(out=woven_half[:].rearrange("p (a i) t -> p a t i", i=RUN), in_=hid[:, c, :, :].rearrange("p t (a i) -> p a t i", i=RUN))
+            return woven_half
 
-        def product2(c, woven):
+        def product2(c, woven_half):
             codes = sb.tile([P, HALF], U32, name="hid_codes%d" % c, align_bytes=64)
             scale = sb.tile([P, HALF], U8, name="hid_scale%d" % c, align_bytes=64)
-            nc.vector.quantize_mx(out=codes[:].bitcast(FP8X4), scales=scale[:], in_=woven[:].rearrange("p a t -> p (a t)"))
-            accs = []
+            nc.vector.quantize_mx(out=codes[:].bitcast(FP8X4), scales=scale[:], in_=woven_half[:].rearrange("p a t -> p (a t)"))
+            banks = []
             for b in range(N // P):
                 rows = slice(b * P, (b + 1) * P)
                 acc = psum.tile([P, HALF], F32, name="acc%d_%d" % (c, b), tag="y%d" % (2 * c + b))
                 nc.tensor.matmul_mx(out=acc[:], lhsT=w2_codes[:, rows].bitcast(FP8X4), lhsT_scale=w2_scale[:, rows],
                                     rhs=codes[:].bitcast(FP8X4), rhs_scale=scale[:], start=True, stop=True)
-                accs.append(acc)
-            return accs
+                banks.append(acc)
+            return banks
 
-        def store(copy, c, b, acc):
+        def store(copy, queue, c, b, acc):
             res = sb.tile([P, HALF], F32, name="res%d_%d" % (c, b))
             copy(res[:], acc[:])
-            nc.sync.dma_start(out=out[b * P:(b + 1) * P, HALVES[c]], in_=res[:])
+            queue.dma_start(out=out[b * P:(b + 1) * P, HALVES[c]], in_=res[:])
 
+        nc.gpsimd.tensor_scalar(w2_dealt[:], w2_raw[:].rearrange("p j n -> p n j"), 1.0, 0.0, ALU.mult, ALU.add)
         rectify(0, False)
         rectify(1, True)
         fetch_and_gate(0)
         rectify(2, True)
         fetch_and_gate(1)
         make_absb(0, ALL)
-        make_child(0, ALL)
         rectify(3, True)
-        rectify(4, False)
+        make_child(0, ALL)
+        rectify(4, True)
         fetch_and_gate(2)
         fetch_and_gate(3)
         make_hid(0, ALL)
         make_absb(1, ALL)
         make_child(1, ALL)
+        nc.vector.quantize_mx(out=w2_codes[:].bitcast(FP8X4), scales=w2_scale[:], in_=w2_dealt[:].rearrange("p n j -> p (n j)"))
         make_absb(2, ALL)
         make_hid(1, ALL)
         make_child(2, ALL)
-        w2_dealt = sb.tile([P, N, PACK], BF16, name="w2_dealt", tag="gate2", align_bytes=64)
-        nc.scalar.copy(out=w2_dealt[:].rearrange("p (a i) j -> p a j i", i=2), in_=w2_raw[:].rearrange("p j (a i) -> p a j i", i=2))
         make_absb(3, ALL)
         woven = []
-        for c in range(2):
+        for c, copy in enumerate((nc.scalar.copy, nc.vector.tensor_copy)):
             make_child(3, HALVES[c])
             make_hid(2, HALVES[c])
             make_hid(3, HALVES[c])
-            if c == 0:
-                woven.append(weave(nc.scalar.copy, 0))
-        nc.vector.quantize_mx(out=w2_codes[:].bitcast(FP8X4), scales=w2_scale[:], in_=w2_dealt[:].rearrange("p n j -> p (n j)"))
-        woven.append(weave(nc.vector.tensor_copy, 1))
+            woven.append(weave(copy, c))
+
         accs = [product2(c, woven[c]) for c in range(2)]
-        for c in range(2):
-            store(nc.scalar.copy, c, 0, accs[c][0])
-            store(nc.vector.tensor_copy, c, 1, accs[c][1])
+        for c, queue in enumerate((nc.sync, nc.scalar)):
+            store(nc.scalar.copy, queue, c, 0, accs[c][0])
+            store(nc.vector.tensor_copy, nc.sync, c, 1, accs[c][1])

from contextlib import ExitStack

import concourse.mybir as mybir

K, T, S, N, H = 1024, 1024, 512, 256, 512
FLOPS = 2 * K * H * S + 2 * H * N * S

F32 = mybir.dt.float32
BF16 = mybir.dt.bfloat16
I32 = mybir.dt.int32
U32 = mybir.dt.uint32
U16 = mybir.dt.uint16
U8 = mybir.dt.uint8
FP8X4 = mybir.dt.float8_e4m3fn_x4
ALU = mybir.AluOpType
ACT = mybir.ActivationFunctionType

P = 128
PACK = 4
K_PASS = P * PACK
PASSES = K // K_PASS
QUADRANT = 32
SCALE_ROWS = 4
LIST_ROWS = 16
SPARE = 32
RUN = 4
HALF = S // 2
ALL = slice(0, S)
HALVES = (slice(0, HALF), slice(HALF, S))


def tile_picked_ysaemt_abs_p_kernel(tc, x_words, x_scales, w1, th1, unit, w2, offs, par, out):
    nc = tc.nc
    with ExitStack() as ctx:
        lists = ctx.enter_context(tc.tile_pool(name="lists", bufs=1))
        sb = ctx.enter_context(tc.tile_pool(name="sb", bufs=1))
        psum = ctx.enter_context(tc.psum_pool(name="psum", bufs=1))

        offs_sb = lists.tile([P, S // LIST_ROWS], U16, name="offs_sb")
        par_sb = lists.tile([P, S // LIST_ROWS], U16, name="par_sb")

        scale_table = sb.tile([P, T], U8, name="scale_table", align_bytes=64)
        nc.gpsimd.memset(scale_table[:].bitcast(I32), 0)
        minus_one = sb.tile([P, 1], F32, name="minus_one")
        nc.gpsimd.memset(minus_one[:], -1.0)
        warm = sb.tile([P, 1], F32, name="warm")
        nc.scalar.activation(warm[:], minus_one[:], ACT.Sigmoid, bias=minus_one[:], scale=4.0)
        ft = [sb.tile([P, S + (SPARE if t else 0)], F32, name="ft%d" % t, align_bytes=64) for t in range(PACK)]
        for t in range(1, PACK):
            nc.gpsimd.memset(ft[t][:, S:], 0.0)
        th_sb = sb.tile([P, PACK], F32, name="th_sb")
        unit_sb = sb.tile([P, PACK], F32, name="unit_sb")
        nc.gpsimd.dma_start(out=th_sb[:], in_=th1.rearrange("(p t) o -> p (t o)", t=PACK))
        nc.gpsimd.dma_start(out=unit_sb[:], in_=unit.rearrange("(p t) o -> p (t o)", t=PACK))
        neg_half_unit = sb.tile([P, PACK], F32, name="neg_half_unit")
        nc.gpsimd.tensor_scalar(neg_half_unit[:], unit_sb[:], -0.5, 0.0, ALU.mult, ALU.add)

        w1_rows = [w1[o * K_PASS:(o + 1) * K_PASS, :].rearrange("(p j) c -> p j c", j=PACK) for o in range(PASSES)]
        w1_raw0 = sb.tile([P, PACK, H], F32, name="w1_raw0")
        word_table = [sb.tile([P, T], U32, name="word_table%d" % o, align_bytes=64) for o in range(PASSES)]
        w1_raw1 = [sb.tile([P, PACK, H // 2], F32, name="w1_raw1_%d" % h) for h in range(2)]
        w2_raw = sb.tile([P, PACK, N], F32, name="w2_raw")

        def load_words(o):
            nc.sync.dma_start(out=word_table[o][:].bitcast(I32), in_=x_words[o].rearrange("p n t -> p (n t)").bitcast(I32))

        load_words(0)
        nc.sync.dma_start(offs_sb[:], offs)
        for q in range(P // QUADRANT):
            nc.sync.dma_start(out=scale_table[QUADRANT * q:QUADRANT * q + SCALE_ROWS * PASSES, :].bitcast(I32),
                              in_=x_scales[:, SCALE_ROWS * q:SCALE_ROWS * (q + 1), :].bitcast(I32))
        nc.sync.dma_start(out=w1_raw0[:], in_=w1_rows[0])
        load_words(1)
        for h in range(2):
            nc.sync.dma_start(out=w1_raw1[h][:], in_=w1_rows[1][:, :, h * (H // 2):(h + 1) * (H // 2)])
        nc.sync.dma_start(par_sb[:], par)
        nc.sync.dma_start(out=w2_raw[:], in_=w2.rearrange("(p j) n -> p j n", j=PACK))

        x_scale = sb.tile([P, S], U8, name="x_scale", align_bytes=64)
        x_codes = [sb.tile([P, S], U32, name="x_codes%d" % o, align_bytes=64) for o in range(PASSES)]
        w1_codes = [sb.tile([P, PACK, P], U32, name="w1_codes%d" % o, align_bytes=64) for o in range(PASSES)]
        w1_scale = [sb.tile([P, PACK, P], U8, name="w1_scale%d" % o, align_bytes=64) for o in range(PASSES)]

        def deal(raw, name):
            m = raw.shape[2] // PACK
            source = raw[:].rearrange("p j (m t) -> p m j t", t=PACK)
            dealt = []
            for pair, copy in enumerate((nc.vector.tensor_copy, nc.scalar.copy)):
                two_slots = sb.tile([P, 2, m, PACK], BF16, name="%s_%d" % (name, pair), align_bytes=64)
                copy(out=two_slots[:].rearrange("p t m j -> p m j t"), in_=source[:, :, :, 2 * pair:2 * pair + 2])
                dealt.append(two_slots)
            return dealt

        nc.vector.tensor_copy(x_codes[0][:], word_table[0][:].indirect(offs_sb[:]))
        nc.vector.tensor_copy(x_scale[:], scale_table[:].indirect(offs_sb[:]))
        dealt0 = deal(w1_raw0, "dealt0")
        for pair in range(2):
            slots = slice(2 * pair, 2 * pair + 2)
            nc.vector.quantize_mx(out=w1_codes[0][:, slots, :].rearrange("p t m -> p (t m)").bitcast(FP8X4),
                                  scales=w1_scale[0][:, slots, :].rearrange("p t m -> p (t m)"),
                                  in_=dealt0[pair][:].rearrange("p t m j -> p (t m j)"))
        nc.vector.tensor_copy(x_codes[1][:], word_table[1][:].indirect(offs_sb[:]))

        pieces = [(0, HALVES[0]), (0, HALVES[1])] + [(t, ALL) for t in range(1, PACK)]
        y = [psum.tile([P, cols.stop - cols.start], F32, name="y%d" % i, tag="y%d" % i) for i, (t, cols) in enumerate(pieces)]

        def product1(o):
            for i, (t, cols) in enumerate(pieces):
                nc.tensor.matmul_mx(out=y[i][:], lhsT=w1_codes[o][:, t, :].bitcast(FP8X4), lhsT_scale=w1_scale[o][:, t, :],
                                    rhs=x_codes[o][:, cols].bitcast(FP8X4), rhs_scale=x_scale[SCALE_ROWS * o:P, cols],
                                    start=(o == 0), stop=(o == PASSES - 1))

        product1(0)
        for h in range(2):
            dealt1 = deal(w1_raw1[h], "dealt1_%d" % h)
            ms = slice(h * (P // 2), (h + 1) * (P // 2))
            for t in range(PACK):
                nc.vector.quantize_mx(out=w1_codes[1][:, t, ms].bitcast(FP8X4), scales=w1_scale[1][:, t, ms],
                                      in_=dealt1[t // 2][:, t % 2, :, :].rearrange("p m j -> p (m j)"))
        product1(1)

        w2_codes = sb.tile([P, N], U32, name="w2_codes", align_bytes=64)
        w2_scale = sb.tile([P, N], U8, name="w2_scale", align_bytes=64)

        fp = [sb.tile([P, S], F32, name="fp%d" % t) for t in range(PACK)]
        gate = [sb.tile([P, S], F32, name="gate%d" % t) for t in range(PACK)]
        absb = [sb.tile([P, S], F32, name="absb%d" % t) for t in range(PACK)]
        child = [sb.tile([P, S], F32, name="child%d" % t) for t in range(PACK)]
        hid = sb.tile([P, 2, PACK, HALF], BF16, name="hid", align_bytes=64)
        w2_dealt = sb.tile([P, N, PACK], BF16, name="w2_dealt", align_bytes=64)

        def rectify(i, on_vector):
            t, cols = pieces[i]
            if on_vector:
                nc.vector.tensor_scalar(ft[t][:, cols], y[i][:], th_sb[:, t:t + 1], 0.0, ALU.add, ALU.max)
            else:
                nc.scalar.activation(ft[t][:, cols], y[i][:], ACT.Relu, bias=th_sb[:, t:t + 1])

        def fetch_and_gate(t):
            if t == 0:
                list_cols = HALF // LIST_ROWS
                nc.scalar.activation(fp[t][:, HALVES[0]], ft[t][:].indirect(par_sb[:, :list_cols]), ACT.Copy)
                nc.vector.tensor_copy(fp[t][:, HALVES[1]], ft[t][:].indirect(par_sb[:, list_cols:]))
            else:
                nc.scalar.activation(fp[t][:], ft[t][:].indirect(par_sb[:]), ACT.Copy)
            nc.scalar.activation(gate[t][:], fp[t][:], ACT.Sigmoid, bias=minus_one[:], scale=4.0)

        def make_absb(t, cols):
            nc.vector.tensor_tensor(absb[t][:, cols], fp[t][:, cols], ft[t][:, cols], ALU.min)

        def make_child(t, cols):
            nc.vector.scalar_tensor_tensor(child[t][:, cols], ft[t][:, cols], unit_sb[:, t:t + 1], gate[t][:, cols], ALU.mult, ALU.mult)

        def make_hid(t, cols):
            halves = slice(cols.start // HALF, cols.stop // HALF)
            nc.vector.scalar_tensor_tensor(hid[:, halves, t, :], absb[t][:, cols].rearrange("p (c j) -> p c j", j=HALF), neg_half_unit[:, t:t + 1],
                                           child[t][:, cols].rearrange("p (c j) -> p c j", j=HALF), ALU.mult, ALU.add)

        def weave(copy, c):
            woven_half = sb.tile([P, HALF, PACK], BF16, name="woven%d" % c, align_bytes=64)
            copy(out=woven_half[:].rearrange("p (a i) t -> p a t i", i=RUN), in_=hid[:, c, :, :].rearrange("p t (a i) -> p a t i", i=RUN))
            return woven_half

        def product2(c, woven_half):
            codes = sb.tile([P, HALF], U32, name="hid_codes%d" % c, align_bytes=64)
            scale = sb.tile([P, HALF], U8, name="hid_scale%d" % c, align_bytes=64)
            nc.vector.quantize_mx(out=codes[:].bitcast(FP8X4), scales=scale[:], in_=woven_half[:].rearrange("p a t -> p (a t)"))
            banks = []
            for b in range(N // P):
                rows = slice(b * P, (b + 1) * P)
                acc = psum.tile([P, HALF], F32, name="acc%d_%d" % (c, b), tag="y%d" % (2 * c + b))
                nc.tensor.matmul_mx(out=acc[:], lhsT=w2_codes[:, rows].bitcast(FP8X4), lhsT_scale=w2_scale[:, rows],
                                    rhs=codes[:].bitcast(FP8X4), rhs_scale=scale[:], start=True, stop=True)
                banks.append(acc)
            return banks

        def store(copy, queue, c, b, acc):
            res = sb.tile([P, HALF], F32, name="res%d_%d" % (c, b))
            copy(res[:], acc[:])
            queue.dma_start(out=out[b * P:(b + 1) * P, HALVES[c]], in_=res[:])

        nc.gpsimd.tensor_scalar(w2_dealt[:], w2_raw[:].rearrange("p j n -> p n j"), 1.0, 0.0, ALU.mult, ALU.add)
        rectify(0, False)
        rectify(1, True)
        fetch_and_gate(0)
        rectify(2, True)
        fetch_and_gate(1)
        make_absb(0, ALL)
        rectify(3, True)
        make_child(0, ALL)
        rectify(4, True)
        fetch_and_gate(2)
        fetch_and_gate(3)
        make_hid(0, ALL)
        make_absb(1, ALL)
        make_child(1, ALL)
        nc.vector.quantize_mx(out=w2_codes[:].bitcast(FP8X4), scales=w2_scale[:], in_=w2_dealt[:].rearrange("p n j -> p (n j)"))
        make_absb(2, ALL)
        make_hid(1, ALL)
        make_child(2, ALL)
        make_absb(3, ALL)
        woven = []
        for c, copy in enumerate((nc.scalar.copy, nc.vector.tensor_copy)):
            make_child(3, HALVES[c])
            make_hid(2, HALVES[c])
            make_hid(3, HALVES[c])
            woven.append(weave(copy, c))

        accs = [product2(c, woven[c]) for c in range(2)]
        for c, queue in enumerate((nc.sync, nc.scalar)):
            store(nc.scalar.copy, queue, c, 0, accs[c][0])
            store(nc.vector.tensor_copy, nc.sync, c, 1, accs[c][1])
